import numpy as np, ml_dtypes
CORES = [242,247,114,119]
N = 4
BF = ml_dtypes.bfloat16
def f(rng, *shape):
    return (rng.standard_normal(shape, dtype=np.float32) * np.exp2(rng.integers(-2, 3, shape[:-1] + (1,)))).astype(BF)
def wide(rng, *shape):
    v = f(rng, *shape).astype(np.float32); k = shape[:-2] + (1, shape[-1])
    return (v * np.exp2(rng.integers(-6, 7, k)) * (rng.random(k) > 0.0625)).astype(BF)
def gentries(a):
    return np.ascontiguousarray(a.reshape(8, 16, -1).transpose(0, 2, 1)).reshape(8, -1)
def gtable(e):
    e = np.asarray(e); return np.ascontiguousarray(e.reshape(8, -1, 16).transpose(0, 2, 1)).reshape(128, -1).astype(np.int32)
S, SH, TL, E, CAP = 4096, 32, 64, 24, 512
D = 256 * SH
def scene(rng):
    v = rng.random((N, 16, D)) ** 2; u = rng.random((N, 16, D)); v = np.where(u < 0.0625, 0.0, np.where(u > 0.96875, 1.0, v))
    o = rng.random((N, 8, S)) ** 2; u = rng.random((N, 8, S)); o = np.where(u < 0.03125, 0.0, np.where(u > 0.9375, 1.0, o))
    m = np.stack([rng.integers(0, SH, (N, 8, S)), rng.integers(0, 8, (N, 8, S)), rng.integers(0, 8, (N, 8, S))], 2).reshape(N, 24, S)
    return {"dic": v.astype(np.float32).astype(BF), "opa": o.astype(np.float32).astype(BF), "hue": f(rng, N, 24, S), "geo": m.astype(np.int32)}
def owners(rng, bias):
    key = rng.random((N, 8, N * CAP)) + np.repeat(bias, CAP, -1)
    w = np.argsort(key, -1)[:, :, :TL * E] // CAP
    return np.take_along_axis(w, np.argsort(rng.random(w.shape), -1), -1)
def lists(w, s, gone):
    e = np.where(gone, -1, w * S + s); return np.stack([gtable(e[r]) for r in range(N)])
def setup_inputs(rng):
    d = scene(rng); w = owners(rng, np.zeros((N, 8, N)))
    d["ent"] = lists(w, rng.integers(0, S, w.shape), rng.random(w.shape) < 0.1); return d
def setup_inputs_full(rng):
    d = scene(rng); r = np.arange(N)[:, None]; g = np.arange(8)[None, :]; bias = np.zeros((N, 8, N))
    bias[r, g, (r + 1 + g % (N - 1)) % N] = -1; bias[r, g[:, 4:], r] = -1
    w = owners(rng, bias); w[:, 1::2] = np.sort(w[:, 1::2], -1)
    whole = np.take_along_axis(bias, w, -1) < 0
    d["ent"] = lists(w, rng.integers(0, S, w.shape), (rng.random(w.shape) < 0.1) & ~whole); return d
def setup_inputs_ends(rng):
    d = scene(rng); b = rng.integers(0, 2, (N, 8, 3, S)) * np.array([SH - 1, 7, 7])[:, None]; d["geo"] = b.reshape(N, 24, S).astype(np.int32)
    r = np.arange(N)[:, None, None, None]; g = np.arange(8)[:, None, None]; t = np.arange(TL)[:, None]; j = np.arange(E)
    w = owners(rng, np.zeros((N, 8, N))).reshape(N, 8, TL, E)
    s = np.where(rng.random((N, 8, TL, 1)) < 0.5, rng.integers(0, 2, (N, 8, TL, E)) * (S - 1), rng.integers(0, S, (N, 8, TL, 1)))
    kind = (r + g + t) % 8
    gone = (kind == 0) | ((kind == 1) & (j > 0)) | ((kind == 2) & (j < E - 1)) | ((kind > 2) & ((rng.random((N, 8, TL, E)) < 0.1) | (w == (r + 1 + g % (N - 1)) % N)))
    gone = gone | ((w == (r + 1 + g % (N - 1)) % N) & (kind < 3))
    gone = gone | (g == r % 8) | ((g == (r + 3) % 8) & (w != (r + 1 + (g + 1) % (N - 1)) % N))
    d["ent"] = lists(w.reshape(N, 8, -1), s.reshape(N, 8, -1), gone.reshape(N, 8, -1)); return d
def setup_inputs_solid(rng):
    d = setup_inputs(rng); u = rng.random((N, 16, D))
    d["dic"] = np.where(u < 0.125, 0.0, np.where(u < 0.25, 1.0, d["dic"].astype(np.float32))).astype(np.float32).astype(BF)
    d["opa"] = np.where(rng.random((N, 8, S)) < 0.5, 1.0, d["opa"].astype(np.float32)).astype(np.float32).astype(BF); return d
def setup_inputs_spread(rng):
    d = scene(rng); d["hue"] = wide(rng, N, 24, S); w = owners(rng, rng.random((N, 8, N)))
    d["ent"] = lists(w, rng.integers(0, S, w.shape), rng.random(w.shape) < 0.1); return d
def check_inputs(d):
    bad = []
    for a in ("dic", "opa"):
        v = d[a].astype(np.float32)
        if not ((v >= 0) & (v <= 1)).all(): bad.append(a + " from 0 to 1")
    if not np.isfinite(d["hue"].astype(np.float32)).all(): bad.append("hue finite")
    m = d["geo"].reshape(N, 8, 3, S)
    if not ((m >= 0).all() and (m[:, :, 0] < SH).all() and (m[:, :, 1:] < 8).all()): bad.append("geo in range")
    e = np.stack([gentries(d["ent"][r]) for r in range(N)])
    if not ((e >= -1) & (e < N * S)).all(): bad.append("ent in range")
    if any((np.sum((e >= q * S) & (e < q * S + S), -1) > CAP).any() for q in range(N)): bad.append("at most CAP entries")
    return bad
def reference(dic, opa, hue, geo, ent):
    y = np.zeros((N, 128, 3 * TL), np.float64); F, O, H = dic.astype(np.float64), opa.astype(np.float64), hue.astype(np.float64)
    g = np.arange(8)[:, None]; t = np.arange(TL * E) // E; tx, ty = t & 7, t >> 3
    for r in range(N):
        e = gentries(ent[r]); k = np.maximum(e, 0).astype(np.int64); q = k // S; s = k - q * S
        at = 256 * geo[q, 3 * g, s] + 16 * (ty - geo[q, 3 * g + 2, s] + 8) + (tx - geo[q, 3 * g + 1, s] + 8)
        a = F[q, :, at] * (O[q, g, s] * (e >= 0))[:, :, None]
        a = a.reshape(8, TL, E, 16); left = np.multiply.accumulate(1 - a, axis=2)
        w = a * np.concatenate([np.ones((8, TL, 1, 16)), left[:, :, :-1]], 2)
        c = H[q[:, :, None], 3 * g[:, :, None] + np.arange(3), s[:, :, None]].reshape(8, TL, E, 3)
        y[r] = np.einsum("gtep,gtec->gpct", w, c).reshape(128, 3 * TL)
    return {"y": y.astype(np.float32)}

@@ -1,0 +1,265 @@
+from concourse.mybir import AluOpType as ALU, ActivationFunctionType as ACT
+
+S, TL, E, D = 4096, 64, 24, 8192
+NE = TL * E
+CH = 384
+CA = 2048
+WA = CA // 8
+WB = (D - CA) // 8
+HOWN = 4
+RESP = 2 * D
+TWW = 2 * S + 32
+
+SCRATCH = {
+    "en": ("sbuf", [128, 96], "int32"), "enr": ("sbuf", [128, 96], "int32"),
+    "g32": ("sbuf", [128, 1024], "int32"),
+    "s1": ("sbuf", [128, 2048], "bfloat16"), "l1": ("sbuf", [128, 2048], "bfloat16"),
+    "pg": ("sbuf", [128, 1024], "bfloat16"), "lg": ("sbuf", [128, 1024], "bfloat16"),
+    "tw": ("sbuf", [128, TWW], "bfloat16"),
+    "dw": ("sbuf", [128, RESP + CH + NE], "bfloat16"),
+    "gtr": ("sbuf", [128, NE], "bfloat16"), "gtl": ("sbuf", [128, NE], "bfloat16"),
+    "ob": ("sbuf", [128, CH + NE], "bfloat16"),
+    "sqm": ("sbuf", [128, CH], "bfloat16"),
+    "fb": ("sbuf", [128, NE], "bfloat16"),
+    "al": ("sbuf", [128, NE], "float32"), "om": ("sbuf", [128, NE], "float32"),
+    "ac": ("sbuf", [128, 3 * NE], "float32"), "sc": ("sbuf", [128, 3 * NE], "float32"),
+    "yb": ("sbuf", [128, 192], "float32"),
+    "xi": ("sbuf", [128, 128], "bfloat16"), "wm": ("sbuf", [128, 1024], "bfloat16"),
+    "cb": ("sbuf", [128, 880], "bfloat16"),
+    "pi": ("sbuf", [128, 8], "int32"), "pf": ("sbuf", [128, 8], "float32"),
+    "tp": ("sbuf", [128, 96], "float32"), "jj": ("sbuf", [128, 96], "float32"),
+    "tlr": ("sbuf", [128, 96], "uint16"), "tll": ("sbuf", [128, 96], "uint16"),
+    "ixr": ("sbuf", [128, 96], "uint16"), "ixl": ("sbuf", [128, 96], "uint16"),
+    "ar": ("sbuf", [128, 96], "float32"), "aa": ("sbuf", [128, 96], "float32"), "ab": ("sbuf", [128, 96], "float32"),
+    "ps": ("psum", [128, 4096], "float32"),
+}
+SEMAPHORES = ["cv", "cs", "cp", "cg", "sent", "a_en", "a_s1", "a_pg", "a_m0", "a_m1", "a_m2",
+              "d_en", "d_geo", "d_s1", "d_dic", "d_tw", "d_y"]
+
+
+def rank_program(g, core, T, topo):
+    rank = T.rank_of(core)
+    if rank is None:
+        return
+    cores = list(T.cores)
+    place = lambda c: (topo.host(c), topo.chip(c))
+    peer = [q for q, c in enumerate(cores) if c != core and place(c) == place(core)][0]
+    cpt = [q for q, c in enumerate(cores) if place(c) != place(core) and topo.die(c) == topo.die(core)][0]
+    assert abs(peer - rank) == 1 and len(cores) == 4
+    lo = S * min(rank, peer)
+    bo, bp = int(rank > peer), int(peer > rank)
+
+    Q = {"g": g, "v": g.vector, "s": g.scalar, "p": g.tensor, "y": g.sync}
+    CS = {"g": "cg", "v": "cv", "s": "cs", "p": "cp"}
+    cnt, seen = {}, {}
+
+    def wait(q, deps):
+        for s, v in deps:
+            if seen.get((q, s), 0) < v:
+                Q[q].wait_ge(T.sem[s], v)
+                seen[(q, s)] = v
+
+    def op(q, deps, f):
+        wait(q, deps)
+        s = CS[q]
+        f(Q[q]).then_inc(T.sem[s], 1)
+        cnt[s] = cnt.get(s, 0) + 1
+        return (s, cnt[s])
+
+    def dma(q, deps, s, out, in_):
+        wait(q, deps)
+        Q[q].dma_start(out, in_).then_inc(T.sem[s], 16)
+        cnt[s] = cnt.get(s, 0) + 16
+        return (s, cnt[s])
+
+    def send(deps, dst, s, out, in_):
+        wait("g", deps)
+        c = cores[dst]
+        rid, pid = topo.addr(c, core)
+        g.remote_dma(out, in_, T.sem[s], T.sem["sent"], pid, rid, topo.mask(core, c))
+        n = len(topo.engines(core, c))
+        cnt["sent"] = cnt.get("sent", 0) + n
+
+    def arrival(src, s):
+        cnt[s] = len(topo.engines(cores[src], core))
+        return (s, cnt[s])
+
+    def mm(deps, parts):
+        wait("p", deps)
+        for i, (o, l, r) in enumerate(parts):
+            ins = g.tensor.matmul(o, l, r, i == 0, i == len(parts) - 1)
+        ins.then_inc(T.sem["cp"], 1)
+        cnt["cp"] = cnt.get("cp", 0) + 1
+        return ("cp", cnt["cp"])
+
+    def copy(q, deps, out, in_):
+        if q == "v":
+            return op(q, deps, lambda e: e.tensor_copy(out, in_))
+        return op(q, deps, lambda e: e.activation(out, in_, ACT.Copy))
+
+    QM, BM, RM = 0, 224, 368
+    two, twp = 16 + S * bo, 16 + S * bp
+    dwo, dwp = D * bo, D * bp
+
+    t_en = dma("s", [], "d_en", T.en[:], T.ent[:])
+    for k in range(4):
+        t_geo = dma("s", [], "d_geo", T.g32[k::4, :], T.geo[k % 3::3, :])
+    dma("y", [], "d_s1", T.s1[:, 1024 + WA:2048], T.dic[:, CA:D])
+    dma("y", [], "d_s1", T.s1[:, 1024:1024 + WA], T.dic[:, 0:CA])
+    dma("y", [], "d_s1", T.s1[0::4, 0:1024], T.opa[:])
+    for c in range(3):
+        t_s1 = dma("y", [], "d_s1", T.s1[1 + c::4, 0:1024], T.hue[c::3, :])
+    co = CA + HOWN * WB
+    for gr in range(4):
+        dma("y", [], "d_dic", T.dw[16 * gr:16 * gr + 16, dwo:dwo + co], T.dic[:, 0:co])
+
+    t_cb = op("v", [], lambda e: e.memset(T.cb[:], 0.0))
+    t_xi = op("g", [], lambda e: e.iota(T.xi[:], [[0, 8], [-8, 16]], 0, 1, allow_small_or_imprecise_dtypes=True))
+    t_pi = op("g", [], lambda e: e.iota(T.pi[:, 0:1], [[0, 1]], 0, 1))
+    t_tp = op("g", [], lambda e: e.iota(T.tp[:], [[16, 8], [2, 4], [0, 3]], 136, 0, allow_small_or_imprecise_dtypes=True))
+    t_jj = op("g", [], lambda e: e.iota(T.jj[:], [[16, 96]], RESP + CH, 0, allow_small_or_imprecise_dtypes=True))
+    qv = T.cb[:, QM + 96:QM + 128]
+    t_q = op("g", [t_cb], lambda e: e.affine_select(qv, qv, [[-16, 8], [-1, 4]], ALU.not_equal, 1.0, -3, 1))
+    bv = T.cb[:, BM + 15:BM + 128:16]
+    t_b = t_q
+    for r, coef in enumerate((256.0, -1.0, -16.0)):
+        t_b = op("g", [t_b], lambda e: e.affine_select(bv, bv, [[-16, 8]], ALU.not_equal, coef, -r, 1))
+    for h in range(8):
+        t_w = op("v", [t_xi], lambda e: e.tensor_scalar(T.wm[:, 128 * h:128 * h + 128], T.xi[:], float(h), None, ALU.is_equal))
+
+    own_lo, own_hi = (0, 16 + S) if bo == 0 else (16 + S, TWW)
+    peer_lo, peer_hi = (0, 16 + S) if bp == 0 else (16 + S, TWW)
+    cut = own_lo + 3072
+    op("v", [], lambda e: e.memset(T.tw[:, own_lo:cut], 0.0))
+    t_pg = copy("v", [t_geo], T.pg[:], T.g32[:])
+    t_zo = op("v", [], lambda e: e.memset(T.tw[:, cut:own_hi], 0.0))
+    t_zp = op("v", [], lambda e: e.memset(T.tw[:, peer_lo:peer_hi], 0.0))
+
+    send([t_en], cpt, "a_en", T.enr[:], T.en[:])
+    send([t_s1], peer, "a_s1", T.l1[:], T.s1[:])
+    send([t_pg], peer, "a_pg", T.lg[:], T.pg[:])
+    a_en, a_s1, a_pg = arrival(cpt, "a_en"), arrival(peer, "a_s1"), arrival(peer, "a_pg")
+    t_r = t_b
+    for h in range(4):
+        rv = T.cb[32 * h:32 * h + 32, RM:RM + 512]
+        t_r = op("g", [t_r], lambda e: e.affine_select(rv, rv, [[-1, 4], [-4, 8], [0, 16]], ALU.not_equal, 1.0, 0, 1))
+
+    dma("y", [t_zo], "d_tw", T.tw[3::16, two:two + S], T.opa[:])
+    for c in range(3):
+        dma("y", [], "d_tw", T.tw[4 + c::16, two:two + S], T.hue[c::3, :])
+    for k in range(3):
+        dma("y", [t_pg], "d_tw", T.tw[k::16, two:two + S], T.pg[k::4, :])
+    for v in range(4):
+        dma("y", [a_s1, t_zp], "d_tw", T.tw[3 + v::16, twp:twp + S], T.l1[v::4, 0:1024])
+    for k in range(3):
+        t_tw = dma("y", [a_pg], "d_tw", T.tw[k::16, twp:twp + S], T.lg[k::4, :])
+    for gr in range(4, 8):
+        dma("y", [], "d_dic", T.dw[16 * gr:16 * gr + 16, dwo:dwo + co], T.dic[:, 0:co])
+    for gr in range(8):
+        t_dic = dma("y", [], "d_dic", T.dw[16 * gr:16 * gr + 16, dwp:dwp + CA], T.l1[:, 1024:1024 + WA])
+
+    t = op("v", [t_pi], lambda e: e.tensor_scalar(T.pi[:, 4:5], T.pi[:, 0:1], 15, None, ALU.bitwise_and))
+    t1 = op("v", [t], lambda e: e.tensor_scalar(T.pf[:, 0:1], T.pi[:, 4:5], 8.0, None, ALU.is_ge))
+    t2 = copy("v", [t], T.pf[:, 4:5], T.pi[:, 4:5])
+    op("v", [t_tp], lambda e: e.tensor_scalar(T.tp[:, 2::3], T.tp[:, 2::3], 1.0, None, ALU.add))
+    t_tp = op("v", [t1], lambda e: e.tensor_scalar(T.tp[:, 1::3], T.tp[:, 1::3], T.pf[:, 0:1], None, ALU.add))
+    t_jj = op("v", [t2, t_jj], lambda e: e.tensor_scalar(T.jj[:], T.jj[:], T.pf[:, 4:5], None, ALU.add))
+    edge, eop = (float(TWW - 16), ALU.min) if lo == 0 else (0.0, ALU.max)
+    t_tll = op("v", [t_en], lambda e: e.tensor_scalar(T.tll[:], T.en[:], float(16 - lo), edge, ALU.add, eop))
+    t_tlr = op("v", [a_en], lambda e: e.tensor_scalar(T.tlr[:], T.enr[:], float(16 - lo), edge, ALU.add, eop))
+    t = op("v", [], lambda e: e.tensor_scalar(T.ar[:], T.enr[:], float(lo + S), float(D), ALU.is_ge, ALU.mult))
+    t_ar = op("v", [t, t_tp], lambda e: e.tensor_tensor(T.ar[:], T.ar[:], T.tp[:], ALU.add))
+
+    free = {}
+    blocks = [("s", T.s1, dwo, h, t_s1) for h in range(HOWN, 8)]
+    blocks += [(q, T.l1, dwp, h, a_s1) for h, q in enumerate("svsvssvs")]
+    turn = {"s": 0, "v": 0}
+    t_dw = {}
+    for q, src, base, h, dep in blocks:
+        slot = (0 if q == "s" else 2) + turn[q] % 2
+        turn[q] += 1
+        p0, c0 = 1024 * slot, 1024 + WA
+        for x in range(0, WB, 512):
+            n = min(512, WB - x)
+            t = mm([dep, t_w] + free.get(slot, []),
+                   [(T.ps[:, p0 + x:p0 + x + n], T.wm[:, 128 * h:128 * h + 128], src[:, c0 + x:c0 + x + n])])
+        w0 = base + CA + WB * h
+        t_dw[q] = copy(q, [t], T.dw[:, w0:w0 + WB], T.ps[:, p0:p0 + WB])
+        free[slot] = [t_dw[q]]
+    dw_all = [t_dw["s"], t_dw["v"], t_dic]
+
+    def gather(q, deps, out, win, off):
+        return copy(q, deps, out, win.indirect(off))
+
+    def wrap(deps, bank, gt):
+        return mm(deps, [(T.ps[:, 512 * bank:512 * bank + 96], T.cb[:, BM + 15 - i:BM + 143 - i], gt[:, i::16]) for i in range(16)])
+
+    def squeeze(deps, bank, gt):
+        return mm(deps, [(T.ps[:, 512 * bank:512 * bank + CH], T.cb[:, QM + 96 - 32 * h:QM + 224 - 32 * h],
+                          gt[:, CH * h:CH * h + CH]) for h in range(4)])
+
+    H = NE // 2
+    t_g0 = gather("v", [t_tw, t_tlr], T.gtr[:, 0:H], T.tw[:, 0:TWW], T.tlr[:, 0:48])
+    t_g1 = gather("s", [t_tw, t_tlr], T.gtr[:, H:NE], T.tw[:, 0:TWW], T.tlr[:, 48:96])
+    t_wr = wrap([t_g0, t_g1, t_b, t_dw["s"], t_dw["v"]], 0, T.gtr)
+    t_sr = squeeze([t_q], 1, T.gtr)
+    t_l1 = gather("s", [t_tll], T.gtl[:, H:NE], T.tw[:, 0:TWW], T.tll[:, 48:96])
+    t = op("v", [], lambda e: e.tensor_scalar(T.aa[:], T.en[:], float(lo + S), float(D), ALU.is_ge, ALU.mult))
+    t1 = op("v", [], lambda e: e.tensor_scalar(T.ab[:], T.en[:], float(2 * S), None, ALU.is_ge if lo == 0 else ALU.is_lt))
+    t = op("v", [t, t_tp], lambda e: e.tensor_tensor(T.aa[:], T.aa[:], T.tp[:], ALU.add))
+    t1 = op("v", [t1, t_jj], lambda e: e.tensor_tensor(T.ab[:], T.ab[:], T.jj[:], ALU.mult))
+    t_aa = op("v", [t, t1], lambda e: e.tensor_tensor(T.aa[:], T.aa[:], T.ab[:], ALU.max))
+    t = op("v", [t_wr, t_ar], lambda e: e.tensor_tensor(T.ar[:], T.ps[:, 0:96], T.ar[:], ALU.add))
+    t_ixr = copy("v", [t], T.ixr[:], T.ar[:])
+    t_sq = copy("s", [t_sr], T.ob[:, 0:CH], T.ps[:, 512:512 + CH])
+    t_f = []
+    for c in range(4):
+        t_f.append(gather("vs"[c % 2], dw_all + [t_ixr], T.ob[:, CH * (c + 1):CH * (c + 2)], T.dw[:, 0:RESP], T.ixr[:, 24 * c:24 * c + 24]))
+    send([t_sq, t_f[0]], cpt, "a_m0", T.dw[:, RESP:RESP + 2 * CH], T.ob[:, 0:2 * CH])
+    send([t_f[1]], cpt, "a_m1", T.dw[:, RESP + 2 * CH:RESP + 3 * CH], T.ob[:, 2 * CH:3 * CH])
+    send([t_f[2], t_f[3]], cpt, "a_m2", T.dw[:, RESP + 3 * CH:RESP + 5 * CH], T.ob[:, 3 * CH:5 * CH])
+    a_m = [arrival(cpt, "a_m0"), arrival(cpt, "a_m1"), arrival(cpt, "a_m2")]
+    a_m.append(a_m[2])
+
+    t_l0 = gather("v", [t_tll], T.gtl[:, 0:H], T.tw[:, 0:TWW], T.tll[:, 0:48])
+    t_wl = wrap([t_l0, t_l1], 2, T.gtl)
+    t_sl = squeeze([], 3, T.gtl)
+    t = op("v", [t_wl, t_aa], lambda e: e.tensor_tensor(T.aa[:], T.ps[:, 1024:1024 + 96], T.aa[:], ALU.add))
+    t_ixl = copy("v", [t], T.ixl[:], T.aa[:])
+    t_sqm = op("v", [t_sl, a_m[0]], lambda e: e.tensor_tensor(T.sqm[:], T.ps[:, 1536:1536 + CH], T.dw[:, RESP:RESP + CH], ALU.add))
+
+    def back(buf, c0):
+        return buf[:, c0 + CH - 1::-1] if c0 == 0 else buf[:, c0 + CH - 1:c0 - 1:-1]
+
+    def fgather(c):
+        hi = RESP + CH * (2, 3, 5, 5)[c]
+        return gather("s", [t_ixl, a_m[c]] + dw_all, T.fb[:, CH * c:CH * c + CH], T.dw[:, 0:hi], T.ixl[:, 24 * c:24 * c + 24])
+
+    def repeat(c, deps):
+        b0 = 4 * ((c + 1) % 2)
+        return [mm(deps, [(T.ps[:, 512 * (b0 + v):512 * (b0 + v) + CH], T.cb[32 * c:32 * c + 32, RM + 128 * v:RM + 128 * v + 128],
+                           T.sqm[32 * c:32 * c + 32, :])]) for v in range(4)]
+
+    t_fb = fgather(0)
+    t_rep = {0: repeat(0, [t_sqm, t_r]), 1: repeat(1, [t_sq, t_ixr, t_ixl])}
+    for c in range(4):
+        c0 = CH * c
+        bank = lambda v: T.ps[:, 512 * (4 * ((c + 1) % 2) + v):512 * (4 * ((c + 1) % 2) + v) + CH]
+        t_a = op("v", [t_fb, t_rep[c][0]], lambda e: e.tensor_tensor(T.al[:, c0:c0 + CH], T.fb[:, c0:c0 + CH], bank(0), ALU.mult))
+        t = op("s", [t_a], lambda e: e.activation(T.om[:, c0:c0 + CH], T.al[:, c0:c0 + CH], ACT.Identity, bias=1.0, scale=-1.0))
+        t_om = op("s", [t], lambda e: e.activation(T.om[:, c0 + E - 1:c0 + CH:E], T.al[:, c0 + E - 1:c0 + CH:E], ACT.Copy, scale=0.0))
+        if c < 3:
+            t_fb = fgather(c + 1)
+        t_ac = []
+        for v in range(3):
+            x0 = NE * v + c0
+            t_ac.append(op("v", [t_a, t_rep[c][1 + v]],
+                           lambda e: e.tensor_tensor(T.ac[:, x0:x0 + CH], T.al[:, c0:c0 + CH], bank(1 + v), ALU.mult)))
+        if c < 2:
+            t_rep[c + 2] = repeat(c + 2, [t_ac[2]])
+        for v in range(3):
+            x0 = NE * v + c0
+            t_sc = op("v", [t_om, t_ac[v]], lambda e: e.tensor_tensor_scan(back(T.sc, x0), back(T.om, c0), back(T.ac, x0), 0.0, ALU.mult, ALU.add))
+    t = copy("v", [t_sc], T.yb[:], T.sc[:, 0::E])
+    dma("y", [t], "d_y", T.y[:], T.yb[:])
+    wait("y", sorted(cnt.items()))

@@ -3,6 +3,8 @@ from concourse.mybir import AluOpType as ALU, ActivationFunctionType as ACT
 S, TL, E, D = 4096, 64, 24, 8192
 NE = TL * E
 CH = 384
+SQ = CH // 4
+MS = SQ + CH
 CA = 2048
 WA = CA // 8
 WB = (D - CA) // 8
@@ -16,16 +18,15 @@ SCRATCH = {
     "s1": ("sbuf", [128, 2048], "bfloat16"), "l1": ("sbuf", [128, 2048], "bfloat16"),
     "pg": ("sbuf", [128, 1024], "bfloat16"), "lg": ("sbuf", [128, 1024], "bfloat16"),
     "tw": ("sbuf", [128, TWW], "bfloat16"),
-    "dw": ("sbuf", [128, RESP + CH + NE], "bfloat16"),
+    "dw": ("sbuf", [128, RESP + 4 * MS], "bfloat16"),
     "gtr": ("sbuf", [128, NE], "bfloat16"), "gtl": ("sbuf", [128, NE], "bfloat16"),
-    "ob": ("sbuf", [128, CH + NE], "bfloat16"),
-    "sqm": ("sbuf", [128, CH], "bfloat16"),
+    "ob": ("sbuf", [128, 4 * MS], "bfloat16"),
     "fb": ("sbuf", [128, NE], "bfloat16"),
     "al": ("sbuf", [128, NE], "float32"), "om": ("sbuf", [128, NE], "float32"),
     "ac": ("sbuf", [128, 3 * NE], "float32"), "sc": ("sbuf", [128, 3 * NE], "float32"),
     "yb": ("sbuf", [128, 192], "float32"),
     "xi": ("sbuf", [128, 128], "bfloat16"), "wm": ("sbuf", [128, 1024], "bfloat16"),
-    "cb": ("sbuf", [128, 880], "bfloat16"),
+    "cb": ("sbuf", [128, 3440], "bfloat16"),
     "pi": ("sbuf", [128, 8], "int32"), "pf": ("sbuf", [128, 8], "float32"),
     "tp": ("sbuf", [128, 96], "float32"), "jj": ("sbuf", [128, 96], "float32"),
     "tlr": ("sbuf", [128, 96], "uint16"), "tll": ("sbuf", [128, 96], "uint16"),
@@ -97,7 +98,7 @@ def rank_program(g, core, T, topo):
             return op(q, deps, lambda e: e.tensor_copy(out, in_))
         return op(q, deps, lambda e: e.activation(out, in_, ACT.Copy))
 
-    QM, BM, RM = 0, 224, 368
+    QM, BM, ZM, LM, RM = 0, 224, 368, 880, 1392
     two, twp = 16 + S * bo, 16 + S * bp
     dwo, dwp = D * bo, D * bp
 
@@ -113,11 +114,11 @@ def rank_program(g, core, T, topo):
     for gr in range(4):
         dma("y", [], "d_dic", T.dw[16 * gr:16 * gr + 16, dwo:dwo + co], T.dic[:, 0:co])
 
-    t_cb = op("v", [], lambda e: e.memset(T.cb[:], 0.0))
+    t_cb = op("v", [], lambda e: e.memset(T.cb[:, 0:ZM], 0.0))
     t_xi = op("g", [], lambda e: e.iota(T.xi[:], [[0, 8], [-8, 16]], 0, 1, allow_small_or_imprecise_dtypes=True))
     t_pi = op("g", [], lambda e: e.iota(T.pi[:, 0:1], [[0, 1]], 0, 1))
     t_tp = op("g", [], lambda e: e.iota(T.tp[:], [[16, 8], [2, 4], [0, 3]], 136, 0, allow_small_or_imprecise_dtypes=True))
-    t_jj = op("g", [], lambda e: e.iota(T.jj[:], [[16, 96]], RESP + CH, 0, allow_small_or_imprecise_dtypes=True))
+    t_jj = op("g", [], lambda e: e.iota(T.jj[:], [[MS, 4], [16, 24]], RESP + SQ, 0, allow_small_or_imprecise_dtypes=True))
     qv = T.cb[:, QM + 96:QM + 128]
     t_q = op("g", [t_cb], lambda e: e.affine_select(qv, qv, [[-16, 8], [-1, 4]], ALU.not_equal, 1.0, -3, 1))
     bv = T.cb[:, BM + 15:BM + 128:16]
@@ -133,16 +134,18 @@ def rank_program(g, core, T, topo):
     op("v", [], lambda e: e.memset(T.tw[:, own_lo:cut], 0.0))
     t_pg = copy("v", [t_geo], T.pg[:], T.g32[:])
     t_zo = op("v", [], lambda e: e.memset(T.tw[:, cut:own_hi], 0.0))
+    t_c2 = op("v", [], lambda e: e.memset(T.cb[:, ZM:LM], 0.0))
     t_zp = op("v", [], lambda e: e.memset(T.tw[:, peer_lo:peer_hi], 0.0))
 
     send([t_en], cpt, "a_en", T.enr[:], T.en[:])
     send([t_s1], peer, "a_s1", T.l1[:], T.s1[:])
     send([t_pg], peer, "a_pg", T.lg[:], T.pg[:])
     a_en, a_s1, a_pg = arrival(cpt, "a_en"), arrival(peer, "a_s1"), arrival(peer, "a_pg")
-    t_r = t_b
+    zv = T.cb[:, ZM:LM]
+    op("g", [t_c2], lambda e: e.affine_select(T.cb[:, LM:RM], zv, [[-1, 4], [-16, 8], [0, 16]], ALU.not_equal, 1.0, -3, 1))
     for h in range(4):
-        rv = T.cb[32 * h:32 * h + 32, RM:RM + 512]
-        t_r = op("g", [t_r], lambda e: e.affine_select(rv, rv, [[-1, 4], [-4, 8], [0, 16]], ALU.not_equal, 1.0, 0, 1))
+        t_r = op("g", [], lambda e: e.affine_select(T.cb[:, RM + 512 * h:RM + 512 * h + 512], zv, [[-1, 4], [-4, 8], [0, 16]],
+                                                    ALU.not_equal, 1.0, -32 * h, 1))
 
     dma("y", [t_zo], "d_tw", T.tw[3::16, two:two + S], T.opa[:])
     for c in range(3):
@@ -159,22 +162,27 @@ def rank_program(g, core, T, topo):
         t_dic = dma("y", [], "d_dic", T.dw[16 * gr:16 * gr + 16, dwp:dwp + CA], T.l1[:, 1024:1024 + WA])
 
     t = op("v", [t_pi], lambda e: e.tensor_scalar(T.pi[:, 4:5], T.pi[:, 0:1], 15, None, ALU.bitwise_and))
-    t1 = op("v", [t], lambda e: e.tensor_scalar(T.pf[:, 0:1], T.pi[:, 4:5], 8.0, None, ALU.is_ge))
-    t2 = copy("v", [t], T.pf[:, 4:5], T.pi[:, 4:5])
     op("v", [t_tp], lambda e: e.tensor_scalar(T.tp[:, 2::3], T.tp[:, 2::3], 1.0, None, ALU.add))
-    t_tp = op("v", [t1], lambda e: e.tensor_scalar(T.tp[:, 1::3], T.tp[:, 1::3], T.pf[:, 0:1], None, ALU.add))
-    t_jj = op("v", [t2, t_jj], lambda e: e.tensor_scalar(T.jj[:], T.jj[:], T.pf[:, 4:5], None, ALU.add))
     edge, eop = (float(TWW - 16), ALU.min) if lo == 0 else (0.0, ALU.max)
     t_tll = op("v", [t_en], lambda e: e.tensor_scalar(T.tll[:], T.en[:], float(16 - lo), edge, ALU.add, eop))
+    t1 = op("v", [t], lambda e: e.tensor_scalar(T.pf[:, 0:1], T.pi[:, 4:5], 8.0, None, ALU.is_ge))
+    t2 = copy("v", [t], T.pf[:, 4:5], T.pi[:, 4:5])
+    t3 = op("v", [], lambda e: e.tensor_scalar(T.aa[:], T.en[:], float(lo + S), float(D), ALU.is_ge, ALU.mult))
+    t4 = op("v", [], lambda e: e.tensor_scalar(T.ab[:], T.en[:], float(2 * S), None, ALU.is_ge if lo == 0 else ALU.is_lt))
+    t_tp = op("v", [t1], lambda e: e.tensor_scalar(T.tp[:, 1::3], T.tp[:, 1::3], T.pf[:, 0:1], None, ALU.add))
+    t_jj = op("v", [t2, t_jj], lambda e: e.tensor_scalar(T.jj[:], T.jj[:], T.pf[:, 4:5], None, ALU.add))
     t_tlr = op("v", [a_en], lambda e: e.tensor_scalar(T.tlr[:], T.enr[:], float(16 - lo), edge, ALU.add, eop))
     t = op("v", [], lambda e: e.tensor_scalar(T.ar[:], T.enr[:], float(lo + S), float(D), ALU.is_ge, ALU.mult))
-    t_ar = op("v", [t, t_tp], lambda e: e.tensor_tensor(T.ar[:], T.ar[:], T.tp[:], ALU.add))
+    t3 = op("v", [t3, t_tp], lambda e: e.tensor_tensor(T.aa[:], T.aa[:], T.tp[:], ALU.add))
+    t4 = op("v", [t4, t_jj], lambda e: e.tensor_tensor(T.ab[:], T.ab[:], T.jj[:], ALU.mult))
+    t_ar = op("v", [t], lambda e: e.tensor_tensor(T.ar[:], T.ar[:], T.tp[:], ALU.add))
+    t_aa = op("v", [t3, t4], lambda e: e.tensor_tensor(T.aa[:], T.aa[:], T.ab[:], ALU.max))
 
-    free = {}
+    free, last = {}, {}
     blocks = [("s", T.s1, dwo, h, t_s1) for h in range(HOWN, 8)]
     blocks += [(q, T.l1, dwp, h, a_s1) for h, q in enumerate("svsvssvs")]
     turn = {"s": 0, "v": 0}
-    t_dw = {}
+    total = {q: sum(b[0] == q for b in blocks) for q in "sv"}
     for q, src, base, h, dep in blocks:
         slot = (0 if q == "s" else 2) + turn[q] % 2
         turn[q] += 1
@@ -184,82 +192,114 @@ def rank_program(g, core, T, topo):
             t = mm([dep, t_w] + free.get(slot, []),
                    [(T.ps[:, p0 + x:p0 + x + n], T.wm[:, 128 * h:128 * h + 128], src[:, c0 + x:c0 + x + n])])
         w0 = base + CA + WB * h
-        t_dw[q] = copy(q, [t], T.dw[:, w0:w0 + WB], T.ps[:, p0:p0 + WB])
-        free[slot] = [t_dw[q]]
-    dw_all = [t_dw["s"], t_dw["v"], t_dic]
+        if turn[q] == total[q]:
+            assert slot % 2 == 0
+            last[q] = ([t], T.dw[:, w0:w0 + WB], T.ps[:, p0:p0 + WB])
+        else:
+            free[slot] = [copy(q, [t], T.dw[:, w0:w0 + WB], T.ps[:, p0:p0 + WB])]
 
-    def gather(q, deps, out, win, off):
-        return copy(q, deps, out, win.indirect(off))
+    def tgather(q, deps, gt, tl, a, b):
+        return copy(q, deps + [t_tw], gt[:, 16 * a:16 * b], T.tw[:, 0:TWW].indirect(tl[:, a:b]))
 
-    def wrap(deps, bank, gt):
-        return mm(deps, [(T.ps[:, 512 * bank:512 * bank + 96], T.cb[:, BM + 15 - i:BM + 143 - i], gt[:, i::16]) for i in range(16)])
+    def wrap(deps, bank, gt, a, b):
+        return mm(deps, [(T.ps[:, 512 * bank:512 * bank + b - a], T.cb[:, BM + 15 - i:BM + 143 - i], gt[:, 16 * a + i:16 * b:16])
+                         for i in range(16)])
 
-    def squeeze(deps, bank, gt):
-        return mm(deps, [(T.ps[:, 512 * bank:512 * bank + CH], T.cb[:, QM + 96 - 32 * h:QM + 224 - 32 * h],
-                          gt[:, CH * h:CH * h + CH]) for h in range(4)])
+    def index(deps, bank, add, ix, a, b):
+        t = op("v", deps, lambda e: e.tensor_tensor(add[:, a:b], T.ps[:, 512 * bank:512 * bank + b - a], add[:, a:b], ALU.add))
+        return copy("v", [t], ix[:, a:b], add[:, a:b])
 
-    H = NE // 2
-    t_g0 = gather("v", [t_tw, t_tlr], T.gtr[:, 0:H], T.tw[:, 0:TWW], T.tlr[:, 0:48])
-    t_g1 = gather("s", [t_tw, t_tlr], T.gtr[:, H:NE], T.tw[:, 0:TWW], T.tlr[:, 48:96])
-    t_wr = wrap([t_g0, t_g1, t_b, t_dw["s"], t_dw["v"]], 0, T.gtr)
-    t_sr = squeeze([t_q], 1, T.gtr)
-    t_l1 = gather("s", [t_tll], T.gtl[:, H:NE], T.tw[:, 0:TWW], T.tll[:, 48:96])
-    t = op("v", [], lambda e: e.tensor_scalar(T.aa[:], T.en[:], float(lo + S), float(D), ALU.is_ge, ALU.mult))
-    t1 = op("v", [], lambda e: e.tensor_scalar(T.ab[:], T.en[:], float(2 * S), None, ALU.is_ge if lo == 0 else ALU.is_lt))
-    t = op("v", [t, t_tp], lambda e: e.tensor_tensor(T.aa[:], T.aa[:], T.tp[:], ALU.add))
-    t1 = op("v", [t1, t_jj], lambda e: e.tensor_tensor(T.ab[:], T.ab[:], T.jj[:], ALU.mult))
-    t_aa = op("v", [t, t1], lambda e: e.tensor_tensor(T.aa[:], T.aa[:], T.ab[:], ALU.max))
-    t = op("v", [t_wr, t_ar], lambda e: e.tensor_tensor(T.ar[:], T.ps[:, 0:96], T.ar[:], ALU.add))
-    t_ixr = copy("v", [t], T.ixr[:], T.ar[:])
-    t_sq = copy("s", [t_sr], T.ob[:, 0:CH], T.ps[:, 512:512 + CH])
-    t_f = []
-    for c in range(4):
-        t_f.append(gather("vs"[c % 2], dw_all + [t_ixr], T.ob[:, CH * (c + 1):CH * (c + 2)], T.dw[:, 0:RESP], T.ixr[:, 24 * c:24 * c + 24]))
-    send([t_sq, t_f[0]], cpt, "a_m0", T.dw[:, RESP:RESP + 2 * CH], T.ob[:, 0:2 * CH])
-    send([t_f[1]], cpt, "a_m1", T.dw[:, RESP + 2 * CH:RESP + 3 * CH], T.ob[:, 2 * CH:3 * CH])
-    send([t_f[2], t_f[3]], cpt, "a_m2", T.dw[:, RESP + 3 * CH:RESP + 5 * CH], T.ob[:, 3 * CH:5 * CH])
+    def squeeze(deps, bank, c):
+        t = mm(deps, [(T.ps[:, 512 * bank:512 * bank + SQ], T.cb[:, QM + 96 - 32 * h:QM + 224 - 32 * h],
+                       T.gtr[:, CH * c + SQ * h:CH * c + SQ * h + SQ]) for h in range(4)])
+        return lambda: copy("s", [t], T.ob[:, MS * c:MS * c + SQ], T.ps[:, 512 * bank:512 * bank + SQ])
+
+    def answer(q, deps, a, b):
+        o = MS * (a // 24) + SQ + 16 * (a % 24)
+        return copy(q, deps + dw_all, T.ob[:, o:o + 16 * (b - a)], T.dw[:, 0:RESP].indirect(T.ixr[:, a:b]))
+
+    r0a = tgather("v", [t_tlr], T.gtr, T.tlr, 0, 12)
+    r0b = tgather("s", [t_tlr], T.gtr, T.tlr, 12, 24)
+    dv, ds = copy("v", *last["v"]), copy("s", *last["s"])
+    dw_all = [dv, ds, t_dic]
+    w0 = wrap([r0a, r0b, t_b] + free[1], 2, T.gtr, 0, 24)
+    q0 = squeeze([t_q], 3, 0)
+    x0 = index([w0, t_ar], 2, T.ar, T.ixr, 0, 24)
+    s0 = q0()
+    f0a, f0b = answer("v", [x0], 0, 12), answer("s", [x0], 12, 24)
+    send([s0, f0a, f0b], cpt, "a_m0", T.dw[:, RESP:RESP + MS], T.ob[:, 0:MS])
+    r1 = tgather("s", [], T.gtr, T.tlr, 24, 48)
+    l0 = tgather("v", [t_tll], T.gtl, T.tll, 0, 24)
+    w1 = wrap([r1] + free[3], 6, T.gtr, 24, 48)
+    q1 = squeeze([], 7, 1)
+    wl0 = wrap([l0, ds], 0, T.gtl, 0, 24)
+    r2 = tgather("s", [], T.gtr, T.tlr, 48, 96)
+    x1 = index([w1], 6, T.ar, T.ixr, 24, 48)
+    f1 = answer("v", [x1], 24, 48)
+    s1 = q1()
+    send([s1, f1], cpt, "a_m1", T.dw[:, RESP + MS:RESP + 2 * MS], T.ob[:, MS:2 * MS])
+    xl0 = index([wl0, t_aa], 0, T.aa, T.ixl, 0, 24)
+    w2 = wrap([r2, dv], 4, T.gtr, 48, 96)
+    q2 = squeeze([], 5, 2)
+    q3 = squeeze([], 1, 3)
+    l1 = tgather("v", [], T.gtl, T.tll, 24, 60)
+    l2 = tgather("s", [t_tll], T.gtl, T.tll, 60, 96)
+    x2 = index([w2], 4, T.ar, T.ixr, 48, 96)
+    s2, s3 = q2(), q3()
+    wl1 = wrap([l1, l2, xl0], 0, T.gtl, 24, 96)
+    f2, f3 = answer("v", [x2], 48, 72), answer("s", [x2], 72, 96)
+    send([s2, s3, f2, f3], cpt, "a_m2", T.dw[:, RESP + 2 * MS:RESP + 4 * MS], T.ob[:, 2 * MS:4 * MS])
+    xl1 = index([wl1], 0, T.aa, T.ixl, 24, 96)
     a_m = [arrival(cpt, "a_m0"), arrival(cpt, "a_m1"), arrival(cpt, "a_m2")]
     a_m.append(a_m[2])
-
-    t_l0 = gather("v", [t_tll], T.gtl[:, 0:H], T.tw[:, 0:TWW], T.tll[:, 0:48])
-    t_wl = wrap([t_l0, t_l1], 2, T.gtl)
-    t_sl = squeeze([], 3, T.gtl)
-    t = op("v", [t_wl, t_aa], lambda e: e.tensor_tensor(T.aa[:], T.ps[:, 1024:1024 + 96], T.aa[:], ALU.add))
-    t_ixl = copy("v", [t], T.ixl[:], T.aa[:])
-    t_sqm = op("v", [t_sl, a_m[0]], lambda e: e.tensor_tensor(T.sqm[:], T.ps[:, 1536:1536 + CH], T.dw[:, RESP:RESP + CH], ALU.add))
 
     def back(buf, c0):
         return buf[:, c0 + CH - 1::-1] if c0 == 0 else buf[:, c0 + CH - 1:c0 - 1:-1]
 
     def fgather(c):
-        hi = RESP + CH * (2, 3, 5, 5)[c]
-        return gather("s", [t_ixl, a_m[c]] + dw_all, T.fb[:, CH * c:CH * c + CH], T.dw[:, 0:hi], T.ixl[:, 24 * c:24 * c + 24])
+        hi = RESP + MS * (1, 2, 4, 4)[c]
+        return copy("s", [xl1 if c else xl0, a_m[c]] + dw_all, T.fb[:, CH * c:CH * c + CH],
+                    T.dw[:, 0:hi].indirect(T.ixl[:, 24 * c:24 * c + 24]))
+
+    BANKS = ((2, 3, 6, 7), (0, 1, 4, 5))
 
     def repeat(c, deps):
-        b0 = 4 * ((c + 1) % 2)
-        return [mm(deps, [(T.ps[:, 512 * (b0 + v):512 * (b0 + v) + CH], T.cb[32 * c:32 * c + 32, RM + 128 * v:RM + 128 * v + 128],
-                           T.sqm[32 * c:32 * c + 32, :])]) for v in range(4)]
+        out = []
+        for v in range(4):
+            p0, r0 = 512 * BANKS[c % 2][v], RESP + MS * c
+            parts = [(T.ps[:, p0:p0 + CH], T.cb[:, LM + 128 * v:LM + 128 * v + 128], T.gtl[:, CH * c:CH * c + CH])]
+            parts += [(T.ps[:, p0 + SQ * h:p0 + SQ * h + SQ], T.cb[:, RM + 512 * h + 128 * v:RM + 512 * h + 128 * v + 128],
+                       T.dw[:, r0:r0 + SQ]) for h in range(4)]
+            out.append(mm(deps + [a_m[c]], parts))
+        return out
 
-    t_fb = fgather(0)
-    t_rep = {0: repeat(0, [t_sqm, t_r]), 1: repeat(1, [t_sq, t_ixr, t_ixl])}
+    def bank(c, v):
+        return T.ps[:, 512 * BANKS[c % 2][v]:512 * BANKS[c % 2][v] + CH]
+
+    def alpha(c):
+        c0 = CH * c
+        t_fb = fgather(c)
+        t_a = op("v", [t_fb, t_rep[c][0]], lambda e: e.tensor_tensor(T.al[:, c0:c0 + CH], T.fb[:, c0:c0 + CH], bank(c, 0), ALU.mult))
+        t = op("s", [t_a], lambda e: e.activation(T.om[:, c0:c0 + CH], T.al[:, c0:c0 + CH], ACT.Identity, bias=1.0, scale=-1.0))
+        return t_a, op("s", [t], lambda e: e.activation(T.om[:, c0 + E - 1:c0 + CH:E], T.al[:, c0 + E - 1:c0 + CH:E], ACT.Copy, scale=0.0))
+
+    t_rep = {0: repeat(0, [t_r, x0, s0, x1, s1]), 1: repeat(1, [xl1, x2, s2, s3])}
+    nxt = alpha(0)
     for c in range(4):
         c0 = CH * c
-        bank = lambda v: T.ps[:, 512 * (4 * ((c + 1) % 2) + v):512 * (4 * ((c + 1) % 2) + v) + CH]
-        t_a = op("v", [t_fb, t_rep[c][0]], lambda e: e.tensor_tensor(T.al[:, c0:c0 + CH], T.fb[:, c0:c0 + CH], bank(0), ALU.mult))
-        t = op("s", [t_a], lambda e: e.activation(T.om[:, c0:c0 + CH], T.al[:, c0:c0 + CH], ACT.Identity, bias=1.0, scale=-1.0))
-        t_om = op("s", [t], lambda e: e.activation(T.om[:, c0 + E - 1:c0 + CH:E], T.al[:, c0 + E - 1:c0 + CH:E], ACT.Copy, scale=0.0))
-        if c < 3:
-            t_fb = fgather(c + 1)
+        t_a, t_om = nxt
         t_ac = []
         for v in range(3):
-            x0 = NE * v + c0
+            z = NE * v + c0
             t_ac.append(op("v", [t_a, t_rep[c][1 + v]],
-                           lambda e: e.tensor_tensor(T.ac[:, x0:x0 + CH], T.al[:, c0:c0 + CH], bank(1 + v), ALU.mult)))
+                           lambda e: e.tensor_tensor(T.ac[:, z:z + CH], T.al[:, c0:c0 + CH], bank(c, 1 + v), ALU.mult)))
         if c < 2:
             t_rep[c + 2] = repeat(c + 2, [t_ac[2]])
+        if c < 3:
+            nxt = alpha(c + 1)
         for v in range(3):
-            x0 = NE * v + c0
-            t_sc = op("v", [t_om, t_ac[v]], lambda e: e.tensor_tensor_scan(back(T.sc, x0), back(T.om, c0), back(T.ac, x0), 0.0, ALU.mult, ALU.add))
+            z = NE * v + c0
+            t_sc = op("v", [t_om, t_ac[v]], lambda e: e.tensor_tensor_scan(back(T.sc, z), back(T.om, c0), back(T.ac, z), 0.0, ALU.mult, ALU.add))
     t = copy("v", [t_sc], T.yb[:], T.sc[:, 0::E])
     dma("y", [t], "d_y", T.y[:], T.yb[:])
     wait("y", sorted(cnt.items()))

from concourse.mybir import AluOpType as ALU, ActivationFunctionType as ACT

S, TL, E, D = 4096, 64, 24, 8192
NE = TL * E
CH = 384
SQ = CH // 4
MS = SQ + CH
CA = 2048
WA = CA // 8
WB = (D - CA) // 8
HOWN = 4
RESP = 2 * D
TWW = 2 * S + 32

SCRATCH = {
    "en": ("sbuf", [128, 96], "int32"), "enr": ("sbuf", [128, 96], "int32"),
    "g32": ("sbuf", [128, 1024], "int32"),
    "s1": ("sbuf", [128, 2048], "bfloat16"), "l1": ("sbuf", [128, 2048], "bfloat16"),
    "pg": ("sbuf", [128, 1024], "bfloat16"), "lg": ("sbuf", [128, 1024], "bfloat16"),
    "tw": ("sbuf", [128, TWW], "bfloat16"),
    "dw": ("sbuf", [128, RESP + 4 * MS], "bfloat16"),
    "gtr": ("sbuf", [128, NE], "bfloat16"), "gtl": ("sbuf", [128, NE], "bfloat16"),
    "ob": ("sbuf", [128, 4 * MS], "bfloat16"),
    "fb": ("sbuf", [128, NE], "bfloat16"),
    "al": ("sbuf", [128, NE], "float32"), "om": ("sbuf", [128, NE], "float32"),
    "ac": ("sbuf", [128, 3 * NE], "float32"), "sc": ("sbuf", [128, 3 * NE], "float32"),
    "yb": ("sbuf", [128, 192], "float32"),
    "xi": ("sbuf", [128, 128], "bfloat16"), "wm": ("sbuf", [128, 1024], "bfloat16"),
    "cb": ("sbuf", [128, 3440], "bfloat16"),
    "pi": ("sbuf", [128, 8], "int32"), "pf": ("sbuf", [128, 8], "float32"),
    "tp": ("sbuf", [128, 96], "float32"), "jj": ("sbuf", [128, 96], "float32"),
    "tlr": ("sbuf", [128, 96], "uint16"), "tll": ("sbuf", [128, 96], "uint16"),
    "ixr": ("sbuf", [128, 96], "uint16"), "ixl": ("sbuf", [128, 96], "uint16"),
    "ar": ("sbuf", [128, 96], "float32"), "aa": ("sbuf", [128, 96], "float32"), "ab": ("sbuf", [128, 96], "float32"),
    "ps": ("psum", [128, 4096], "float32"),
}
SEMAPHORES = ["cv", "cs", "cp", "cg", "sent", "a_en", "a_s1", "a_pg", "a_m0", "a_m1", "a_m2",
              "d_en", "d_geo", "d_s1", "d_dic", "d_tw", "d_y"]


def rank_program(g, core, T, topo):
    rank = T.rank_of(core)
    if rank is None:
        return
    cores = list(T.cores)
    place = lambda c: (topo.host(c), topo.chip(c))
    peer = [q for q, c in enumerate(cores) if c != core and place(c) == place(core)][0]
    cpt = [q for q, c in enumerate(cores) if place(c) != place(core) and topo.die(c) == topo.die(core)][0]
    assert abs(peer - rank) == 1 and len(cores) == 4
    lo = S * min(rank, peer)
    bo, bp = int(rank > peer), int(peer > rank)

    Q = {"g": g, "v": g.vector, "s": g.scalar, "p": g.tensor, "y": g.sync}
    CS = {"g": "cg", "v": "cv", "s": "cs", "p": "cp"}
    cnt, seen = {}, {}

    def wait(q, deps):
        for s, v in deps:
            if seen.get((q, s), 0) < v:
                Q[q].wait_ge(T.sem[s], v)
                seen[(q, s)] = v

    def op(q, deps, f):
        wait(q, deps)
        s = CS[q]
        f(Q[q]).then_inc(T.sem[s], 1)
        cnt[s] = cnt.get(s, 0) + 1
        return (s, cnt[s])

    def dma(q, deps, s, out, in_):
        wait(q, deps)
        Q[q].dma_start(out, in_).then_inc(T.sem[s], 16)
        cnt[s] = cnt.get(s, 0) + 16
        return (s, cnt[s])

    def send(deps, dst, s, out, in_):
        wait("g", deps)
        c = cores[dst]
        rid, pid = topo.addr(c, core)
        g.remote_dma(out, in_, T.sem[s], T.sem["sent"], pid, rid, topo.mask(core, c))
        n = len(topo.engines(core, c))
        cnt["sent"] = cnt.get("sent", 0) + n

    def arrival(src, s):
        cnt[s] = len(topo.engines(cores[src], core))
        return (s, cnt[s])

    def mm(deps, parts):
        wait("p", deps)
        for i, (o, l, r) in enumerate(parts):
            ins = g.tensor.matmul(o, l, r, i == 0, i == len(parts) - 1)
        ins.then_inc(T.sem["cp"], 1)
        cnt["cp"] = cnt.get("cp", 0) + 1
        return ("cp", cnt["cp"])

    def copy(q, deps, out, in_):
        if q == "v":
            return op(q, deps, lambda e: e.tensor_copy(out, in_))
        return op(q, deps, lambda e: e.activation(out, in_, ACT.Copy))

    QM, BM, ZM, LM, RM = 0, 224, 368, 880, 1392
    two, twp = 16 + S * bo, 16 + S * bp
    dwo, dwp = D * bo, D * bp

    t_en = dma("s", [], "d_en", T.en[:], T.ent[:])
    for k in range(4):
        t_geo = dma("s", [], "d_geo", T.g32[k::4, :], T.geo[k % 3::3, :])
    dma("y", [], "d_s1", T.s1[:, 1024 + WA:2048], T.dic[:, CA:D])
    dma("y", [], "d_s1", T.s1[:, 1024:1024 + WA], T.dic[:, 0:CA])
    dma("y", [], "d_s1", T.s1[0::4, 0:1024], T.opa[:])
    for c in range(3):
        t_s1 = dma("y", [], "d_s1", T.s1[1 + c::4, 0:1024], T.hue[c::3, :])
    co = CA + HOWN * WB
    for gr in range(4):
        dma("y", [], "d_dic", T.dw[16 * gr:16 * gr + 16, dwo:dwo + co], T.dic[:, 0:co])

    t_cb = op("v", [], lambda e: e.memset(T.cb[:, 0:ZM], 0.0))
    t_xi = op("g", [], lambda e: e.iota(T.xi[:], [[0, 8], [-8, 16]], 0, 1, allow_small_or_imprecise_dtypes=True))
    t_pi = op("g", [], lambda e: e.iota(T.pi[:, 0:1], [[0, 1]], 0, 1))
    t_tp = op("g", [], lambda e: e.iota(T.tp[:], [[16, 8], [2, 4], [0, 3]], 136, 0, allow_small_or_imprecise_dtypes=True))
    t_jj = op("g", [], lambda e: e.iota(T.jj[:], [[MS, 4], [16, 24]], RESP + SQ, 0, allow_small_or_imprecise_dtypes=True))
    qv = T.cb[:, QM + 96:QM + 128]
    t_q = op("g", [t_cb], lambda e: e.affine_select(qv, qv, [[-16, 8], [-1, 4]], ALU.not_equal, 1.0, -3, 1))
    bv = T.cb[:, BM + 15:BM + 128:16]
    t_b = t_q
    for r, coef in enumerate((256.0, -1.0, -16.0)):
        t_b = op("g", [t_b], lambda e: e.affine_select(bv, bv, [[-16, 8]], ALU.not_equal, coef, -r, 1))
    for h in range(8):
        t_w = op("v", [t_xi], lambda e: e.tensor_scalar(T.wm[:, 128 * h:128 * h + 128], T.xi[:], float(h), None, ALU.is_equal))

    own_lo, own_hi = (0, 16 + S) if bo == 0 else (16 + S, TWW)
    peer_lo, peer_hi = (0, 16 + S) if bp == 0 else (16 + S, TWW)
    cut = own_lo + 3072
    op("v", [], lambda e: e.memset(T.tw[:, own_lo:cut], 0.0))
    t_pg = copy("v", [t_geo], T.pg[:], T.g32[:])
    t_zo = op("v", [], lambda e: e.memset(T.tw[:, cut:own_hi], 0.0))
    t_c2 = op("v", [], lambda e: e.memset(T.cb[:, ZM:LM], 0.0))
    t_zp = op("v", [], lambda e: e.memset(T.tw[:, peer_lo:peer_hi], 0.0))

    send([t_en], cpt, "a_en", T.enr[:], T.en[:])
    send([t_s1], peer, "a_s1", T.l1[:], T.s1[:])
    send([t_pg], peer, "a_pg", T.lg[:], T.pg[:])
    a_en, a_s1, a_pg = arrival(cpt, "a_en"), arrival(peer, "a_s1"), arrival(peer, "a_pg")
    zv = T.cb[:, ZM:LM]
    op("g", [t_c2], lambda e: e.affine_select(T.cb[:, LM:RM], zv, [[-1, 4], [-16, 8], [0, 16]], ALU.not_equal, 1.0, -3, 1))
    for h in range(4):
        t_r = op("g", [], lambda e: e.affine_select(T.cb[:, RM + 512 * h:RM + 512 * h + 512], zv, [[-1, 4], [-4, 8], [0, 16]],
                                                    ALU.not_equal, 1.0, -32 * h, 1))

    dma("y", [t_zo], "d_tw", T.tw[3::16, two:two + S], T.opa[:])
    for c in range(3):
        dma("y", [], "d_tw", T.tw[4 + c::16, two:two + S], T.hue[c::3, :])
    for k in range(3):
        dma("y", [t_pg], "d_tw", T.tw[k::16, two:two + S], T.pg[k::4, :])
    for v in range(4):
        dma("y", [a_s1, t_zp], "d_tw", T.tw[3 + v::16, twp:twp + S], T.l1[v::4, 0:1024])
    for k in range(3):
        t_tw = dma("y", [a_pg], "d_tw", T.tw[k::16, twp:twp + S], T.lg[k::4, :])
    for gr in range(4, 8):
        dma("y", [], "d_dic", T.dw[16 * gr:16 * gr + 16, dwo:dwo + co], T.dic[:, 0:co])
    for gr in range(8):
        t_dic = dma("y", [], "d_dic", T.dw[16 * gr:16 * gr + 16, dwp:dwp + CA], T.l1[:, 1024:1024 + WA])

    t = op("v", [t_pi], lambda e: e.tensor_scalar(T.pi[:, 4:5], T.pi[:, 0:1], 15, None, ALU.bitwise_and))
    op("v", [t_tp], lambda e: e.tensor_scalar(T.tp[:, 2::3], T.tp[:, 2::3], 1.0, None, ALU.add))
    edge, eop = (float(TWW - 16), ALU.min) if lo == 0 else (0.0, ALU.max)
    t_tll = op("v", [t_en], lambda e: e.tensor_scalar(T.tll[:], T.en[:], float(16 - lo), edge, ALU.add, eop))
    t1 = op("v", [t], lambda e: e.tensor_scalar(T.pf[:, 0:1], T.pi[:, 4:5], 8.0, None, ALU.is_ge))
    t2 = copy("v", [t], T.pf[:, 4:5], T.pi[:, 4:5])
    t3 = op("v", [], lambda e: e.tensor_scalar(T.aa[:], T.en[:], float(lo + S), float(D), ALU.is_ge, ALU.mult))
    t4 = op("v", [], lambda e: e.tensor_scalar(T.ab[:], T.en[:], float(2 * S), None, ALU.is_ge if lo == 0 else ALU.is_lt))
    t_tp = op("v", [t1], lambda e: e.tensor_scalar(T.tp[:, 1::3], T.tp[:, 1::3], T.pf[:, 0:1], None, ALU.add))
    t_jj = op("v", [t2, t_jj], lambda e: e.tensor_scalar(T.jj[:], T.jj[:], T.pf[:, 4:5], None, ALU.add))
    t_tlr = op("v", [a_en], lambda e: e.tensor_scalar(T.tlr[:], T.enr[:], float(16 - lo), edge, ALU.add, eop))
    t = op("v", [], lambda e: e.tensor_scalar(T.ar[:], T.enr[:], float(lo + S), float(D), ALU.is_ge, ALU.mult))
    t3 = op("v", [t3, t_tp], lambda e: e.tensor_tensor(T.aa[:], T.aa[:], T.tp[:], ALU.add))
    t4 = op("v", [t4, t_jj], lambda e: e.tensor_tensor(T.ab[:], T.ab[:], T.jj[:], ALU.mult))
    t_ar = op("v", [t], lambda e: e.tensor_tensor(T.ar[:], T.ar[:], T.tp[:], ALU.add))
    t_aa = op("v", [t3, t4], lambda e: e.tensor_tensor(T.aa[:], T.aa[:], T.ab[:], ALU.max))

    free, last = {}, {}
    blocks = [("s", T.s1, dwo, h, t_s1) for h in range(HOWN, 8)]
    blocks += [(q, T.l1, dwp, h, a_s1) for h, q in enumerate("svsvssvs")]
    turn = {"s": 0, "v": 0}
    total = {q: sum(b[0] == q for b in blocks) for q in "sv"}
    for q, src, base, h, dep in blocks:
        slot = (0 if q == "s" else 2) + turn[q] % 2
        turn[q] += 1
        p0, c0 = 1024 * slot, 1024 + WA
        for x in range(0, WB, 512):
            n = min(512, WB - x)
            t = mm([dep, t_w] + free.get(slot, []),
                   [(T.ps[:, p0 + x:p0 + x + n], T.wm[:, 128 * h:128 * h + 128], src[:, c0 + x:c0 + x + n])])
        w0 = base + CA + WB * h
        if turn[q] == total[q]:
            assert slot % 2 == 0
            last[q] = ([t], T.dw[:, w0:w0 + WB], T.ps[:, p0:p0 + WB])
        else:
            free[slot] = [copy(q, [t], T.dw[:, w0:w0 + WB], T.ps[:, p0:p0 + WB])]

    def tgather(q, deps, gt, tl, a, b):
        return copy(q, deps + [t_tw], gt[:, 16 * a:16 * b], T.tw[:, 0:TWW].indirect(tl[:, a:b]))

    def wrap(deps, bank, gt, a, b):
        return mm(deps, [(T.ps[:, 512 * bank:512 * bank + b - a], T.cb[:, BM + 15 - i:BM + 143 - i], gt[:, 16 * a + i:16 * b:16])
                         for i in range(16)])

    def index(deps, bank, add, ix, a, b):
        t = op("v", deps, lambda e: e.tensor_tensor(add[:, a:b], T.ps[:, 512 * bank:512 * bank + b - a], add[:, a:b], ALU.add))
        return copy("v", [t], ix[:, a:b], add[:, a:b])

    def squeeze(deps, bank, c):
        t = mm(deps, [(T.ps[:, 512 * bank:512 * bank + SQ], T.cb[:, QM + 96 - 32 * h:QM + 224 - 32 * h],
                       T.gtr[:, CH * c + SQ * h:CH * c + SQ * h + SQ]) for h in range(4)])
        return lambda: copy("s", [t], T.ob[:, MS * c:MS * c + SQ], T.ps[:, 512 * bank:512 * bank + SQ])

    def answer(q, deps, a, b):
        o = MS * (a // 24) + SQ + 16 * (a % 24)
        return copy(q, deps + dw_all, T.ob[:, o:o + 16 * (b - a)], T.dw[:, 0:RESP].indirect(T.ixr[:, a:b]))

    r0a = tgather("v", [t_tlr], T.gtr, T.tlr, 0, 12)
    r0b = tgather("s", [t_tlr], T.gtr, T.tlr, 12, 24)
    dv, ds = copy("v", *last["v"]), copy("s", *last["s"])
    dw_all = [dv, ds, t_dic]
    w0 = wrap([r0a, r0b, t_b] + free[1], 2, T.gtr, 0, 24)
    q0 = squeeze([t_q], 3, 0)
    x0 = index([w0, t_ar], 2, T.ar, T.ixr, 0, 24)
    s0 = q0()
    f0a, f0b = answer("v", [x0], 0, 12), answer("s", [x0], 12, 24)
    send([s0, f0a, f0b], cpt, "a_m0", T.dw[:, RESP:RESP + MS], T.ob[:, 0:MS])
    r1 = tgather("s", [], T.gtr, T.tlr, 24, 48)
    l0 = tgather("v", [t_tll], T.gtl, T.tll, 0, 24)
    w1 = wrap([r1] + free[3], 6, T.gtr, 24, 48)
    q1 = squeeze([], 7, 1)
    wl0 = wrap([l0, ds], 0, T.gtl, 0, 24)
    r2 = tgather("s", [], T.gtr, T.tlr, 48, 96)
    x1 = index([w1], 6, T.ar, T.ixr, 24, 48)
    f1 = answer("v", [x1], 24, 48)
    s1 = q1()
    send([s1, f1], cpt, "a_m1", T.dw[:, RESP + MS:RESP + 2 * MS], T.ob[:, MS:2 * MS])
    xl0 = index([wl0, t_aa], 0, T.aa, T.ixl, 0, 24)
    w2 = wrap([r2, dv], 4, T.gtr, 48, 96)
    q2 = squeeze([], 5, 2)
    q3 = squeeze([], 1, 3)
    l1 = tgather("v", [], T.gtl, T.tll, 24, 60)
    l2 = tgather("s", [t_tll], T.gtl, T.tll, 60, 96)
    x2 = index([w2], 4, T.ar, T.ixr, 48, 96)
    s2, s3 = q2(), q3()
    wl1 = wrap([l1, l2, xl0], 0, T.gtl, 24, 96)
    f2, f3 = answer("v", [x2], 48, 72), answer("s", [x2], 72, 96)
    send([s2, s3, f2, f3], cpt, "a_m2", T.dw[:, RESP + 2 * MS:RESP + 4 * MS], T.ob[:, 2 * MS:4 * MS])
    xl1 = index([wl1], 0, T.aa, T.ixl, 24, 96)
    a_m = [arrival(cpt, "a_m0"), arrival(cpt, "a_m1"), arrival(cpt, "a_m2")]
    a_m.append(a_m[2])

    def back(buf, c0):
        return buf[:, c0 + CH - 1::-1] if c0 == 0 else buf[:, c0 + CH - 1:c0 - 1:-1]

    def fgather(c):
        hi = RESP + MS * (1, 2, 4, 4)[c]
        return copy("s", [xl1 if c else xl0, a_m[c]] + dw_all, T.fb[:, CH * c:CH * c + CH],
                    T.dw[:, 0:hi].indirect(T.ixl[:, 24 * c:24 * c + 24]))

    BANKS = ((2, 3, 6, 7), (0, 1, 4, 5))

    def repeat(c, deps):
        out = []
        for v in range(4):
            p0, r0 = 512 * BANKS[c % 2][v], RESP + MS * c
            parts = [(T.ps[:, p0:p0 + CH], T.cb[:, LM + 128 * v:LM + 128 * v + 128], T.gtl[:, CH * c:CH * c + CH])]
            parts += [(T.ps[:, p0 + SQ * h:p0 + SQ * h + SQ], T.cb[:, RM + 512 * h + 128 * v:RM + 512 * h + 128 * v + 128],
                       T.dw[:, r0:r0 + SQ]) for h in range(4)]
            out.append(mm(deps + [a_m[c]], parts))
        return out

    def bank(c, v):
        return T.ps[:, 512 * BANKS[c % 2][v]:512 * BANKS[c % 2][v] + CH]

    def alpha(c):
        c0 = CH * c
        t_fb = fgather(c)
        t_a = op("v", [t_fb, t_rep[c][0]], lambda e: e.tensor_tensor(T.al[:, c0:c0 + CH], T.fb[:, c0:c0 + CH], bank(c, 0), ALU.mult))
        t = op("s", [t_a], lambda e: e.activation(T.om[:, c0:c0 + CH], T.al[:, c0:c0 + CH], ACT.Identity, bias=1.0, scale=-1.0))
        return t_a, op("s", [t], lambda e: e.activation(T.om[:, c0 + E - 1:c0 + CH:E], T.al[:, c0 + E - 1:c0 + CH:E], ACT.Copy, scale=0.0))

    t_rep = {0: repeat(0, [t_r, x0, s0, x1, s1]), 1: repeat(1, [xl1, x2, s2, s3])}
    nxt = alpha(0)
    for c in range(4):
        c0 = CH * c
        t_a, t_om = nxt
        t_ac = []
        for v in range(3):
            z = NE * v + c0
            t_ac.append(op("v", [t_a, t_rep[c][1 + v]],
                           lambda e: e.tensor_tensor(T.ac[:, z:z + CH], T.al[:, c0:c0 + CH], bank(c, 1 + v), ALU.mult)))
        if c < 2:
            t_rep[c + 2] = repeat(c + 2, [t_ac[2]])
        if c < 3:
            nxt = alpha(c + 1)
        for v in range(3):
            z = NE * v + c0
            t_sc = op("v", [t_om, t_ac[v]], lambda e: e.tensor_tensor_scan(back(T.sc, z), back(T.om, c0), back(T.ac, z), 0.0, ALU.mult, ALU.add))
    t = copy("v", [t_sc], T.yb[:], T.sc[:, 0::E])
    dma("y", [t], "d_y", T.y[:], T.yb[:])
    wait("y", sorted(cnt.items()))
